import numpy as np
import ml_dtypes


def mxq(x, axis, fmt="e4m3"):
    dtype, down = {"e4m3": (ml_dtypes.float8_e4m3fn, 7), "e5m2": (ml_dtypes.float8_e5m2, 14)}[fmt]
    v = np.moveaxis(np.asarray(x, np.float32).astype(ml_dtypes.bfloat16).astype(np.float64), axis, -1)
    blocks = v.reshape(v.shape[:-1] + (-1, 32))
    amax = np.abs(blocks).max(-1, keepdims=True)
    byte = np.maximum(np.where(amax > 0, np.frexp(amax)[1] - 1 + 127, 0) - down, 1)
    scale = np.exp2(byte - 127.0)
    codes = (blocks / scale).astype(np.float32).astype(dtype).astype(np.float64)
    return np.moveaxis((codes * scale).reshape(v.shape), -1, axis)


WIDE = False


def mx_kscale(k):
    if not WIDE:
        return np.ones(k)
    levels = np.array([10, -10, 5, -5, 0])
    if k % 512:
        return np.exp2(np.random.permutation(np.resize(levels, k // 32))).repeat(32)
    a = np.empty((k // 512, 16))
    for p in range(k // 512):
        a[p, :8] = np.random.permutation(np.resize(levels, 8))
        for g in range(8):
            far = levels[np.abs(levels - a[p, g]) >= 10]
            a[p, g + 8] = far[np.random.randint(len(far))]
    return np.exp2(a.ravel()).repeat(32)


def f64(x):
    return np.asarray(x).astype(np.float64)


def striped8(idx):
    return np.asarray(idx).reshape(8, -1, 16).transpose(0, 2, 1).reshape(128, -1).astype(np.uint16)


def unstriped8(offs):
    return offs.reshape(8, 16, -1).transpose(0, 2, 1).reshape(8, -1).astype(np.int64)


def pick8(x, idx, run):
    r = np.arange(len(x))
    return x[r[:, None], idx[r % (8 * run) // run]]


E2M1 = np.array([0.0, 0.5, 1.0, 1.5, 2.0, 3.0, 4.0, 6.0, -0.0, -0.5, -1.0, -1.5, -2.0, -3.0, -4.0, -6.0])


def pack_weight(w, fmt):
    k, n = w.shape
    w = f64(np.asarray(w, np.float32).astype(ml_dtypes.bfloat16)).reshape(k // 32, 32, n)
    amax = np.abs(w).max(1)
    if fmt == "e4m3":
        byte = np.frexp(amax)[1] - 1 + 127 - 7
    else:
        mant, ex = np.frexp(amax / 6.0)
        byte = np.where(mant > 0.5, ex, ex - 1) + 127
    byte = np.clip(np.where(amax > 0, byte, 1), 1, 254)
    scaled = (w * np.exp2(127.0 - byte)[:, None, :]).reshape(k, n).astype(np.float32)
    by_word = np.ascontiguousarray(scaled.reshape(k // 512, 128, 4, n).transpose(0, 1, 3, 2))
    if fmt == "e4m3":
        words = by_word.astype(ml_dtypes.float8_e4m3fn).view(np.uint8)
    else:
        c = by_word.astype(ml_dtypes.float4_e2m1fn).view(np.uint8) & 0xF
        words = (c[..., 0::2] | (c[..., 1::2] << 4)).reshape(k // 512, 128, 2 * n)
    return np.ascontiguousarray(words), np.ascontiguousarray(byte.astype(np.uint8).reshape(k // 512, 16, n))


def unpack_weight(words, scales, fmt):
    g, _, n = scales.shape
    words = np.ascontiguousarray(words).reshape(g, 128, n, -1)
    if fmt == "e4m3":
        vals = words.view(ml_dtypes.float8_e4m3fn).astype(np.float64)
    else:
        nib = np.empty((g, 128, n, 4), np.uint8)
        nib[..., 0::2] = words & 0xF
        nib[..., 1::2] = words >> 4
        vals = E2M1[nib]
    vals = vals * np.repeat(np.exp2(scales.astype(np.float64) - 127.0), 8, axis=1)[..., None]
    return vals.transpose(0, 1, 3, 2).reshape(g * 512, n)


def softplus(v):
    return np.log(1.0 + np.exp(v))


def sigmoid(v):
    return 1.0 / (1.0 + np.exp(-v))


D, E, T, Q, I = 512, 512, 1024, 128, 512


def setup_inputs():
    n = np.random.standard_normal
    idx = np.stack([np.random.permutation(T)[:I] for _ in range(8)])
    fd = mx_kscale(D)
    fe = mx_kscale(E)
    keysp = pack_weight(n((D, T)) / fd[:, None], "e2m1")
    return {
        "query": (n((D, Q)) * 1.0 / np.sqrt(D) * fd[:, None]).astype(np.float32),
        "keys_words": keysp[0],
        "keys_scales": keysp[1],
        "gout": (n((E, Q)) * 1 / np.sqrt(E) * fe[:, None]).astype(np.float32),
        "vals": (n((E, T)) / fe[:, None]).astype(np.float32),
        "th": (np.random.uniform(-0.5, 0.5, (Q, 1))).astype(np.float32),
        "reserve": (np.random.uniform(20.0, 60.0, (Q, 1))).astype(np.float32),
        "dquery": (n((D, Q)) * 1.0 / np.sqrt(D) * fd[:, None]).astype(np.float32),
        "base": (0.5 * n((Q, T))).astype(np.float32),
        "offs": striped8(idx),
    }


def reference(query, keys_words, keys_scales, gout, vals, th, reserve, dquery, base, offs):
    idx = unstriped8(offs)
    keysu = unpack_weight(keys_words, keys_scales, "e2m1")
    queryq = mxq(f64(query), 0, "e4m3")
    a = queryq.T @ keysu
    dqueryq = mxq(f64(dquery), 0, "e4m3")
    ta = dqueryq.T @ keysu
    p = softplus(pick8(a, idx, 16) - f64(th))
    z = np.sum(p, axis=1, keepdims=True) + f64(reserve)
    goutq = mxq(f64(gout), 0, "e4m3")
    valsq = mxq(f64(vals), 0, "e4m3")
    c0 = goutq.T @ valsq
    dw = pick8(c0, idx, 16)
    dz = np.sum(dw * p / np.square(z) * (-1.0), axis=1, keepdims=True)
    dp = dw / z + dz
    xp = pick8(ta, idx, 16) * sigmoid(pick8(a, idx, 16) - f64(th))
    xz = np.sum(xp, axis=1, keepdims=True)
    xdz = np.sum((xp * dw - xz * z * 2.0 * dw * p / np.square(z)) / np.square(z) * (-1.0), axis=1, keepdims=True)
    xdp = xz * dw / np.square(z) * (-1.0) + xdz
    xe1 = xdp * sigmoid(pick8(a, idx, 16) - f64(th)) + pick8(ta, idx, 16) * sigmoid(pick8(a, idx, 16) - f64(th)) * (1.0 - sigmoid(pick8(a, idx, 16) - f64(th))) * dp
    xs1 = np.zeros((Q, T))
    xs1[np.arange(Q)[:, None], idx[np.arange(Q) % 128 // 16]] = xe1
    y = xs1 * 1024.0 + f64(base)
    return y

@@ -1,0 +1,195 @@
+from contextlib import ExitStack
+
+import concourse.mybir as mybir
+
+D, E, T, Q, I = 512, 512, 1024, 128, 512
+FLOPS = 3 * 2 * D * Q * T
+
+F32 = mybir.dt.float32
+BF16 = mybir.dt.bfloat16
+I32 = mybir.dt.int32
+U32 = mybir.dt.uint32
+U16 = mybir.dt.uint16
+U8 = mybir.dt.uint8
+FP8X4 = mybir.dt.float8_e4m3fn_x4
+FP4X4 = mybir.dt.float4_e2m1fn_x4
+ALU = mybir.AluOpType
+ACT = mybir.ActivationFunctionType
+
+P = 128
+PACK = 4
+BANK = 512
+CHUNK = 256
+
+
+def tile_attend_hvspotlight_heads_kernel(tc, query, keys_words, keys_scales, gout, vals, th, reserve, dquery, base, offs, out):
+    nc = tc.nc
+    with ExitStack() as ctx:
+        sb = ctx.enter_context(tc.tile_pool(name="sb", bufs=1))
+        ps = ctx.enter_context(tc.psum_pool(name="ps", bufs=1))
+
+        def load_rows(name, src):
+            raw = sb.tile([P, PACK, src.shape[1]], F32, name=name + "_raw", align_bytes=64)
+            nc.sync.dma_start(out=raw[:], in_=src.rearrange("(p j) w -> p j w", j=PACK))
+            return raw
+
+        def weave(name, raw, on_scalar):
+            width = raw.shape[2]
+            woven = sb.tile([P, width, PACK], BF16, name=name + "_bf", align_bytes=64)
+            dst = woven[:].rearrange("p (c i) j -> p c j i", i=4)
+            src = raw[:].rearrange("p j (c i) -> p c j i", i=4)
+            if on_scalar:
+                nc.scalar.copy(out=dst, in_=src)
+            else:
+                nc.vector.tensor_copy(out=dst, in_=src)
+            return woven
+
+        def quantise(name, woven):
+            width = woven.shape[1]
+            codes = sb.tile([P, width], U32, name=name + "_codes", align_bytes=64)
+            scales = sb.tile([P, width], U8, name=name + "_scales", align_bytes=64)
+            nc.vector.quantize_mx(out=codes[:].bitcast(FP8X4), scales=scales[:], in_=woven[:].rearrange("p w j -> p (w j)"))
+            return codes, scales
+
+        def column(name):
+            return sb.tile([P, 1], F32, name=name)
+
+        def slots(name):
+            return sb.tile([P, I], F32, name=name, align_bytes=64)
+
+        warm = column("warm")
+        warm_out = column("warm_out")
+        nc.vector.memset(warm[:], 0.0)
+        nc.scalar.activation(out=warm_out[:], in_=warm[:], func=ACT.Sigmoid)
+
+        key_scales = sb.tile([P, T], U8, name="key_scales", align_bytes=64)
+        nc.vector.memset(key_scales[:].bitcast(I32), 0)
+        for quad in range(4):
+            nc.scalar.dma_start(
+                out=key_scales[32 * quad : 32 * quad + 4, :].bitcast(I32),
+                in_=keys_scales[0, 4 * quad : 4 * quad + 4, :].bitcast(I32),
+            )
+        q_raw = load_rows("q", query)
+        key_words = sb.tile([P, 2 * T], U8, name="key_words", align_bytes=64)
+        nc.sync.dma_start(out=key_words[:].bitcast(I32), in_=keys_words[0].bitcast(I32))
+        dq_raw = load_rows("dq", dquery)
+        g_raw = load_rows("gout", gout)
+        lists = sb.tile([P, I // 16], U16, name="lists")
+        nc.sync.dma_start(lists[:], offs)
+        v_raw = [load_rows("v%d" % c, vals[:, c * CHUNK : (c + 1) * CHUNK]) for c in range(T // CHUNK)]
+        base_sb = sb.tile([P, T], F32, name="base_sb")
+        nc.sync.dma_start(out=base_sb[:], in_=base)
+
+        th_sb = column("th_sb")
+        reserve_sb = column("reserve_sb")
+        nc.gpsimd.dma_start(out=th_sb[:], in_=th)
+        nc.gpsimd.dma_start(out=reserve_sb[:], in_=reserve)
+        placed = sb.tile([P, T], F32, name="placed")
+        nc.gpsimd.memset(placed[:], 0.0)
+        neg_th = column("neg_th")
+        nc.gpsimd.tensor_scalar(neg_th[:], th_sb[:], -1.0, 0.0, ALU.mult, ALU.add)
+
+        def scores(name, codes, scales, second_on_vector):
+            whole = sb.tile([P, T], F32, name=name)
+            for h in range(T // BANK):
+                bank = ps.tile([P, BANK], F32, name="%s_bank%d" % (name, h))
+                nc.tensor.matmul_mx(
+                    out=bank[:],
+                    lhsT=codes[:].bitcast(FP8X4),
+                    lhsT_scale=scales[:],
+                    rhs=key_words[:, 2 * h * BANK : 2 * (h + 1) * BANK].bitcast(FP4X4),
+                    rhs_scale=key_scales[:, h * BANK : (h + 1) * BANK],
+                    start=True,
+                    stop=True,
+                )
+                if h == 1 and second_on_vector:
+                    nc.vector.tensor_copy(out=whole[:, h * BANK : (h + 1) * BANK], in_=bank[:])
+                else:
+                    nc.scalar.copy(out=whole[:, h * BANK : (h + 1) * BANK], in_=bank[:])
+            return whole
+
+        q_bf = weave("q", q_raw, False)
+        q_codes, q_scales = quantise("q", q_bf)
+        dq_bf = weave("dq", dq_raw, True)
+        dq_codes, dq_scales = quantise("dq", dq_bf)
+        g_bf = weave("gout", g_raw, False)
+        a_all = scores("a", q_codes, q_scales, True)
+        g_codes, g_scales = quantise("gout", g_bf)
+        ta_all = scores("ta", dq_codes, dq_scales, False)
+
+        a_list = slots("a_list")
+        nc.vector.tensor_copy(a_list[:], a_all[:].indirect(lists[:]))
+        sig = slots("sig")
+        nc.scalar.activation(out=sig[:], in_=a_list[:], func=ACT.Sigmoid, bias=neg_th[:])
+        fold = slots("fold")
+        nc.scalar.activation(out=fold[:], in_=sig[:], func=ACT.Abs, bias=-0.5)
+        log_part = slots("log_part")
+        log_sum = column("log_sum")
+        nc.scalar.activation(out=log_part[:], in_=fold[:], func=ACT.Ln, bias=0.5, accum_out=log_sum[:])
+        ramp = slots("ramp")
+        ramp_sum = column("ramp_sum")
+        nc.scalar.activation(out=ramp[:], in_=a_list[:], func=ACT.Relu, bias=neg_th[:], accum_out=ramp_sum[:])
+
+        c0_all = sb.tile([P, T], F32, name="c0_all")
+
+        def value_chunk(c, on_scalar):
+            v_bf = weave("v%d" % c, v_raw[c], on_scalar)
+            v_codes, v_scales = quantise("v%d" % c, v_bf)
+            bank = ps.tile([P, CHUNK], F32, name="c0_bank%d" % c)
+            nc.tensor.matmul_mx(
+                out=bank[:],
+                lhsT=g_codes[:].bitcast(FP8X4),
+                lhsT_scale=g_scales[:],
+                rhs=v_codes[:].bitcast(FP8X4),
+                rhs_scale=v_scales[:],
+                start=True,
+                stop=True,
+            )
+            nc.scalar.copy(out=c0_all[:, c * CHUNK : (c + 1) * CHUNK], in_=bank[:])
+
+        value_chunk(0, True)
+        ta_list = slots("ta_list")
+        nc.vector.tensor_copy(ta_list[:], ta_all[:].indirect(lists[:]))
+        value_chunk(1, False)
+        neg_xp = slots("neg_xp")
+        neg_xz = column("neg_xz")
+        nc.vector.scalar_tensor_tensor(neg_xp[:], ta_list[:], -1.0, sig[:], ALU.mult, ALU.mult, accum_out=neg_xz[:])
+        value_chunk(2, True)
+        curve = slots("curve")
+        nc.vector.scalar_tensor_tensor(curve[:], sig[:], 1.0, neg_xp[:], ALU.subtract, ALU.mult)
+        value_chunk(3, False)
+
+        z_part = column("z_part")
+        nc.vector.tensor_scalar(z_part[:], ramp_sum[:], reserve_sb[:], log_sum[:], ALU.add, ALU.subtract)
+        neg_p = slots("neg_p")
+        nc.vector.tensor_tensor(neg_p[:], log_part[:], ramp[:], ALU.subtract)
+        inv_z = column("inv_z")
+        nc.vector.reciprocal(inv_z[:], z_part[:])
+        dw = slots("dw")
+        nc.vector.tensor_copy(dw[:], c0_all[:].indirect(lists[:]))
+        xz_share = column("xz_share")
+        nc.vector.tensor_scalar(xz_share[:], neg_xz[:], inv_z[:], None, ALU.mult)
+        row_scale = column("row_scale")
+        nc.scalar.activation(out=row_scale[:], in_=inv_z[:], func=ACT.Copy, scale=1024.0)
+
+        scrap_a = slots("scrap_a")
+        shift = column("shift")
+        nc.vector.scalar_tensor_tensor(scrap_a[:], neg_p[:], inv_z[:], dw[:], ALU.mult, ALU.mult, accum_out=shift[:])
+        scrap_b = slots("scrap_b")
+        b_share = column("b_share")
+        nc.vector.scalar_tensor_tensor(scrap_b[:], neg_xp[:], inv_z[:], dw[:], ALU.mult, ALU.mult, accum_out=b_share[:])
+        slope = slots("slope")
+        nc.vector.scalar_tensor_tensor(slope[:], sig[:], xz_share[:], curve[:], ALU.mult, ALU.add)
+        offset = column("offset")
+        nc.scalar.activation(out=offset[:], in_=shift[:], func=ACT.Identity, scale=xz_share[:], bias=b_share[:])
+        level = slots("level")
+        nc.scalar.activation(out=level[:], in_=sig[:], func=ACT.Copy, scale=offset[:])
+        main = slots("main")
+        nc.vector.scalar_tensor_tensor(main[:], dw[:], shift[:], slope[:], ALU.add, ALU.mult)
+        nc.vector.tensor_tensor(placed[:].indirect(lists[:]), main[:], level[:], ALU.add)
+
+        for h in range(T // BANK):
+            cols = slice(h * BANK, (h + 1) * BANK)
+            result = sb.tile([P, BANK], F32, name="result%d" % h)
+            nc.vector.scalar_tensor_tensor(result[:], placed[:, cols], row_scale[:], base_sb[:, cols], ALU.mult, ALU.add)
+            nc.sync.dma_start(out=out[:, cols], in_=result[:])

@@ -29,13 +29,13 @@ def tile_attend_hvspotlight_heads_kernel(tc, query, keys_words, keys_scales, gou
         ps = ctx.enter_context(tc.psum_pool(name="ps", bufs=1))
 
         def load_rows(name, src):
-            raw = sb.tile([P, PACK, src.shape[1]], F32, name=name + "_raw", align_bytes=64)
+            raw = sb.tile([P, PACK, src.shape[1]], F32, name=name + "_raw", tag=name + "_raw", align_bytes=64)
             nc.sync.dma_start(out=raw[:], in_=src.rearrange("(p j) w -> p j w", j=PACK))
             return raw
 
-        def weave(name, raw, on_scalar):
+        def weave(name, raw, on_scalar, tag=None):
             width = raw.shape[2]
-            woven = sb.tile([P, width, PACK], BF16, name=name + "_bf", align_bytes=64)
+            woven = sb.tile([P, width, PACK], BF16, name=name + "_bf", tag=tag or name + "_bf", align_bytes=64)
             dst = woven[:].rearrange("p (c i) j -> p c j i", i=4)
             src = raw[:].rearrange("p j (c i) -> p c j i", i=4)
             if on_scalar:
@@ -44,53 +44,53 @@ def tile_attend_hvspotlight_heads_kernel(tc, query, keys_words, keys_scales, gou
                 nc.vector.tensor_copy(out=dst, in_=src)
             return woven
 
-        def quantise(name, woven):
+        def quantise(name, woven, tag=None):
             width = woven.shape[1]
-            codes = sb.tile([P, width], U32, name=name + "_codes", align_bytes=64)
+            codes = sb.tile([P, width], U32, name=name + "_codes", tag=tag or name + "_codes", align_bytes=64)
             scales = sb.tile([P, width], U8, name=name + "_scales", align_bytes=64)
             nc.vector.quantize_mx(out=codes[:].bitcast(FP8X4), scales=scales[:], in_=woven[:].rearrange("p w j -> p (w j)"))
             return codes, scales
 
-        def column(name):
-            return sb.tile([P, 1], F32, name=name)
+        def column(name, tag=None):
+            return sb.tile([P, 1], F32, name=name, tag=tag or name, align_bytes=64)
 
-        def slots(name):
-            return sb.tile([P, I], F32, name=name, align_bytes=64)
-
-        warm = column("warm")
-        warm_out = column("warm_out")
-        nc.vector.memset(warm[:], 0.0)
-        nc.scalar.activation(out=warm_out[:], in_=warm[:], func=ACT.Sigmoid)
+        def slots(name, tag=None):
+            return sb.tile([P, I], F32, name=name, tag=tag or name, align_bytes=64)
 
         key_scales = sb.tile([P, T], U8, name="key_scales", align_bytes=64)
         nc.vector.memset(key_scales[:].bitcast(I32), 0)
         for quad in range(4):
-            nc.scalar.dma_start(
+            nc.sync.dma_start(
                 out=key_scales[32 * quad : 32 * quad + 4, :].bitcast(I32),
                 in_=keys_scales[0, 4 * quad : 4 * quad + 4, :].bitcast(I32),
             )
+        warm = column("warm")
+        warm_out = column("warm_out")
+        nc.vector.memset(warm[:], 0.0)
+        nc.scalar.activation(out=warm_out[:], in_=warm[:], func=ACT.Sigmoid)
         q_raw = load_rows("q", query)
         key_words = sb.tile([P, 2 * T], U8, name="key_words", align_bytes=64)
         nc.sync.dma_start(out=key_words[:].bitcast(I32), in_=keys_words[0].bitcast(I32))
         dq_raw = load_rows("dq", dquery)
-        g_raw = load_rows("gout", gout)
+        v_raw = [load_rows("v0", vals[:, 0:CHUNK])]
         lists = sb.tile([P, I // 16], U16, name="lists")
         nc.sync.dma_start(lists[:], offs)
-        v_raw = [load_rows("v%d" % c, vals[:, c * CHUNK : (c + 1) * CHUNK]) for c in range(T // CHUNK)]
+        g_raw = load_rows("gout", gout)
+        th_sb = column("th_sb")
+        nc.sync.dma_start(out=th_sb[:], in_=th)
+        v_raw.extend(load_rows("v%d" % c, vals[:, c * CHUNK : (c + 1) * CHUNK]) for c in range(1, T // CHUNK))
+        reserve_sb = column("reserve_sb")
+        nc.sync.dma_start(out=reserve_sb[:], in_=reserve)
         base_sb = sb.tile([P, T], F32, name="base_sb")
         nc.sync.dma_start(out=base_sb[:], in_=base)
 
-        th_sb = column("th_sb")
-        reserve_sb = column("reserve_sb")
-        nc.gpsimd.dma_start(out=th_sb[:], in_=th)
-        nc.gpsimd.dma_start(out=reserve_sb[:], in_=reserve)
         placed = sb.tile([P, T], F32, name="placed")
-        nc.gpsimd.memset(placed[:], 0.0)
+        nc.vector.memset(placed[:], 0.0)
         neg_th = column("neg_th")
-        nc.gpsimd.tensor_scalar(neg_th[:], th_sb[:], -1.0, 0.0, ALU.mult, ALU.add)
+        nc.scalar.activation(out=neg_th[:], in_=th_sb[:], func=ACT.Copy, scale=-1.0)
 
         def scores(name, codes, scales, second_on_vector):
-            whole = sb.tile([P, T], F32, name=name)
+            whole = sb.tile([P, T], F32, name=name, tag=name, align_bytes=64)
             for h in range(T // BANK):
                 bank = ps.tile([P, BANK], F32, name="%s_bank%d" % (name, h))
                 nc.tensor.matmul_mx(
@@ -108,33 +108,9 @@ def tile_attend_hvspotlight_heads_kernel(tc, query, keys_words, keys_scales, gou
                     nc.scalar.copy(out=whole[:, h * BANK : (h + 1) * BANK], in_=bank[:])
             return whole
 
-        q_bf = weave("q", q_raw, False)
-        q_codes, q_scales = quantise("q", q_bf)
-        dq_bf = weave("dq", dq_raw, True)
-        dq_codes, dq_scales = quantise("dq", dq_bf)
-        g_bf = weave("gout", g_raw, False)
-        a_all = scores("a", q_codes, q_scales, True)
-        g_codes, g_scales = quantise("gout", g_bf)
-        ta_all = scores("ta", dq_codes, dq_scales, False)
+        c0_all = sb.tile([P, T], F32, name="c0_all", tag="c0_all", align_bytes=64)
 
-        a_list = slots("a_list")
-        nc.vector.tensor_copy(a_list[:], a_all[:].indirect(lists[:]))
-        sig = slots("sig")
-        nc.scalar.activation(out=sig[:], in_=a_list[:], func=ACT.Sigmoid, bias=neg_th[:])
-        fold = slots("fold")
-        nc.scalar.activation(out=fold[:], in_=sig[:], func=ACT.Abs, bias=-0.5)
-        log_part = slots("log_part")
-        log_sum = column("log_sum")
-        nc.scalar.activation(out=log_part[:], in_=fold[:], func=ACT.Ln, bias=0.5, accum_out=log_sum[:])
-        ramp = slots("ramp")
-        ramp_sum = column("ramp_sum")
-        nc.scalar.activation(out=ramp[:], in_=a_list[:], func=ACT.Relu, bias=neg_th[:], accum_out=ramp_sum[:])
-
-        c0_all = sb.tile([P, T], F32, name="c0_all")
-
-        def value_chunk(c, on_scalar):
-            v_bf = weave("v%d" % c, v_raw[c], on_scalar)
-            v_codes, v_scales = quantise("v%d" % c, v_bf)
+        def value_scores(c, v_codes, v_scales):
             bank = ps.tile([P, CHUNK], F32, name="c0_bank%d" % c)
             nc.tensor.matmul_mx(
                 out=bank[:],
@@ -147,49 +123,68 @@ def tile_attend_hvspotlight_heads_kernel(tc, query, keys_words, keys_scales, gou
             )
             nc.scalar.copy(out=c0_all[:, c * CHUNK : (c + 1) * CHUNK], in_=bank[:])
 
-        value_chunk(0, True)
-        ta_list = slots("ta_list")
-        nc.vector.tensor_copy(ta_list[:], ta_all[:].indirect(lists[:]))
-        value_chunk(1, False)
-        neg_xp = slots("neg_xp")
-        neg_xz = column("neg_xz")
-        nc.vector.scalar_tensor_tensor(neg_xp[:], ta_list[:], -1.0, sig[:], ALU.mult, ALU.mult, accum_out=neg_xz[:])
-        value_chunk(2, True)
-        curve = slots("curve")
-        nc.vector.scalar_tensor_tensor(curve[:], sig[:], 1.0, neg_xp[:], ALU.subtract, ALU.mult)
-        value_chunk(3, False)
+        q_bf = weave("q", q_raw, False)
+        q_codes, q_scales = quantise("q", q_bf)
+        a_all = scores("a", q_codes, q_scales, False)
+        dq_bf = weave("dq", dq_raw, False)
+        dq_codes, dq_scales = quantise("dq", dq_bf)
 
-        z_part = column("z_part")
-        nc.vector.tensor_scalar(z_part[:], ramp_sum[:], reserve_sb[:], log_sum[:], ALU.add, ALU.subtract)
-        neg_p = slots("neg_p")
+        a_list = slots("a_list")
+        nc.vector.tensor_copy(a_list[:], a_all[:].indirect(lists[:]))
+        sig = slots("sig")
+        nc.scalar.activation(out=sig[:], in_=a_list[:], func=ACT.Sigmoid, bias=neg_th[:])
+        ta_all = scores("ta", dq_codes, dq_scales, False)
+        g_bf = weave("gout", g_raw, False)
+        fold = slots("fold")
+        nc.scalar.activation(out=fold[:], in_=sig[:], func=ACT.Abs, bias=-0.5)
+        ramp = slots("ramp")
+        ramp_sum = column("ramp_sum")
+        nc.scalar.activation(out=ramp[:], in_=a_list[:], func=ACT.Relu, bias=neg_th[:], accum_out=ramp_sum[:])
+        log_part = slots("log_part")
+        log_sum = column("log_sum")
+        nc.scalar.activation(out=log_part[:], in_=fold[:], func=ACT.Ln, bias=0.5, accum_out=log_sum[:])
+        z_known = column("z_known")
+        nc.scalar.activation(out=z_known[:], in_=ramp_sum[:], func=ACT.Identity, bias=reserve_sb[:])
+        z_row = column("z_row")
+        nc.scalar.activation(out=z_row[:], in_=log_sum[:], func=ACT.Identity, scale=-1.0, bias=z_known[:])
+
+        g_codes, g_scales = quantise("gout", g_bf)
+        value_scores(0, *quantise("v0", weave("v0", v_raw[0], False)))
+        v_bf = [None] + [weave("v%d" % c, v_raw[c], False) for c in range(1, T // CHUNK)]
+        value_scores(1, *quantise("v1", v_bf[1], tag="v2_raw"))
+        value_scores(2, *quantise("v2", v_bf[2], tag="v3_raw"))
+        value_scores(3, *quantise("v3", v_bf[3]))
+        xp = slots("xp", tag="v3_bf")
+        nc.vector.tensor_tensor(xp[:], ta_all[:].indirect(lists[:]), sig[:], ALU.mult)
+        inv_z = column("inv_z", tag="ta")
+        nc.vector.reciprocal(inv_z[:], z_row[:])
+        neg_p = slots("neg_p", tag="v2_bf")
         nc.vector.tensor_tensor(neg_p[:], log_part[:], ramp[:], ALU.subtract)
-        inv_z = column("inv_z")
-        nc.vector.reciprocal(inv_z[:], z_part[:])
+        xp_share = slots("xp_share")
+        xz_share = column("xz_share")
+        nc.scalar.activation(out=xp_share[:], in_=xp[:], func=ACT.Copy, scale=inv_z[:], accum_out=xz_share[:])
+        row_scale = column("row_scale")
+        nc.scalar.activation(out=row_scale[:], in_=inv_z[:], func=ACT.Copy, scale=-1024.0)
+
         dw = slots("dw")
         nc.vector.tensor_copy(dw[:], c0_all[:].indirect(lists[:]))
-        xz_share = column("xz_share")
-        nc.vector.tensor_scalar(xz_share[:], neg_xz[:], inv_z[:], None, ALU.mult)
-        row_scale = column("row_scale")
-        nc.scalar.activation(out=row_scale[:], in_=inv_z[:], func=ACT.Copy, scale=1024.0)
-
+        neg_curve = slots("neg_curve", tag="c0_all")
+        nc.vector.scalar_tensor_tensor(neg_curve[:], sig[:], 1.0, xp[:], ALU.subtract, ALU.mult)
         scrap_a = slots("scrap_a")
         shift = column("shift")
         nc.vector.scalar_tensor_tensor(scrap_a[:], neg_p[:], inv_z[:], dw[:], ALU.mult, ALU.mult, accum_out=shift[:])
-        scrap_b = slots("scrap_b")
-        b_share = column("b_share")
-        nc.vector.scalar_tensor_tensor(scrap_b[:], neg_xp[:], inv_z[:], dw[:], ALU.mult, ALU.mult, accum_out=b_share[:])
         slope = slots("slope")
-        nc.vector.scalar_tensor_tensor(slope[:], sig[:], xz_share[:], curve[:], ALU.mult, ALU.add)
+        nc.vector.scalar_tensor_tensor(slope[:], sig[:], xz_share[:], neg_curve[:], ALU.mult, ALU.add)
+        scrap_b = slots("scrap_b")
         offset = column("offset")
-        nc.scalar.activation(out=offset[:], in_=shift[:], func=ACT.Identity, scale=xz_share[:], bias=b_share[:])
+        nc.vector.scalar_tensor_tensor(scrap_b[:], dw[:], shift[:], xp_share[:], ALU.add, ALU.mult, accum_out=offset[:])
         level = slots("level")
         nc.scalar.activation(out=level[:], in_=sig[:], func=ACT.Copy, scale=offset[:])
         main = slots("main")
         nc.vector.scalar_tensor_tensor(main[:], dw[:], shift[:], slope[:], ALU.add, ALU.mult)
         nc.vector.tensor_tensor(placed[:].indirect(lists[:]), main[:], level[:], ALU.add)
 
-        for h in range(T // BANK):
-            cols = slice(h * BANK, (h + 1) * BANK)
-            result = sb.tile([P, BANK], F32, name="result%d" % h)
+        for h, cols in enumerate((slice(0, 512), slice(512, 768), slice(768, 1024))):
+            result = sb.tile([P, cols.stop - cols.start], F32, name="result%d" % h)
             nc.vector.scalar_tensor_tensor(result[:], placed[:, cols], row_scale[:], base_sb[:, cols], ALU.mult, ALU.add)
             nc.sync.dma_start(out=out[:, cols], in_=result[:])

@@ -33,15 +33,15 @@ def tile_attend_hvspotlight_heads_kernel(tc, query, keys_words, keys_scales, gou
             nc.sync.dma_start(out=raw[:], in_=src.rearrange("(p j) w -> p j w", j=PACK))
             return raw
 
-        def weave(name, raw, on_scalar, tag=None):
+        def weave(name, raw, scalar_columns=0):
             width = raw.shape[2]
-            woven = sb.tile([P, width, PACK], BF16, name=name + "_bf", tag=tag or name + "_bf", align_bytes=64)
+            woven = sb.tile([P, width, PACK], BF16, name=name + "_bf", tag=name + "_bf", align_bytes=64)
             dst = woven[:].rearrange("p (c i) j -> p c j i", i=4)
             src = raw[:].rearrange("p j (c i) -> p c j i", i=4)
-            if on_scalar:
-                nc.scalar.copy(out=dst, in_=src)
-            else:
-                nc.vector.tensor_copy(out=dst, in_=src)
+            cut = scalar_columns // 4
+            if cut:
+                nc.scalar.copy(out=dst[:, :cut], in_=src[:, :cut])
+            nc.vector.tensor_copy(out=dst[:, cut:], in_=src[:, cut:])
             return woven
 
         def quantise(name, woven, tag=None):
@@ -72,10 +72,10 @@ def tile_attend_hvspotlight_heads_kernel(tc, query, keys_words, keys_scales, gou
         key_words = sb.tile([P, 2 * T], U8, name="key_words", align_bytes=64)
         nc.sync.dma_start(out=key_words[:].bitcast(I32), in_=keys_words[0].bitcast(I32))
         dq_raw = load_rows("dq", dquery)
+        g_raw = load_rows("gout", gout)
         v_raw = [load_rows("v0", vals[:, 0:CHUNK])]
         lists = sb.tile([P, I // 16], U16, name="lists")
         nc.sync.dma_start(lists[:], offs)
-        g_raw = load_rows("gout", gout)
         th_sb = column("th_sb")
         nc.sync.dma_start(out=th_sb[:], in_=th)
         v_raw.extend(load_rows("v%d" % c, vals[:, c * CHUNK : (c + 1) * CHUNK]) for c in range(1, T // CHUNK))
@@ -110,10 +110,12 @@ def tile_attend_hvspotlight_heads_kernel(tc, query, keys_words, keys_scales, gou
 
         c0_all = sb.tile([P, T], F32, name="c0_all", tag="c0_all", align_bytes=64)
 
+        c0_banks = [ps.tile([P, BANK], F32, name="c0_bank%d" % h) for h in range(T // BANK)]
+
         def value_scores(c, v_codes, v_scales):
-            bank = ps.tile([P, CHUNK], F32, name="c0_bank%d" % c)
+            h, part = divmod(c * CHUNK, BANK)
             nc.tensor.matmul_mx(
-                out=bank[:],
+                out=c0_banks[h][:, part : part + CHUNK],
                 lhsT=g_codes[:].bitcast(FP8X4),
                 lhsT_scale=g_scales[:],
                 rhs=v_codes[:].bitcast(FP8X4),
@@ -121,55 +123,60 @@ def tile_attend_hvspotlight_heads_kernel(tc, query, keys_words, keys_scales, gou
                 start=True,
                 stop=True,
             )
-            nc.scalar.copy(out=c0_all[:, c * CHUNK : (c + 1) * CHUNK], in_=bank[:])
 
-        q_bf = weave("q", q_raw, False)
+        q_bf = weave("q", q_raw)
         q_codes, q_scales = quantise("q", q_bf)
         a_all = scores("a", q_codes, q_scales, False)
-        dq_bf = weave("dq", dq_raw, False)
+        dq_bf = weave("dq", dq_raw)
+        g_bf = weave("gout", g_raw)
         dq_codes, dq_scales = quantise("dq", dq_bf)
+        g_codes, g_scales = quantise("gout", g_bf)
 
         a_list = slots("a_list")
-        nc.vector.tensor_copy(a_list[:], a_all[:].indirect(lists[:]))
-        sig = slots("sig")
-        nc.scalar.activation(out=sig[:], in_=a_list[:], func=ACT.Sigmoid, bias=neg_th[:])
+        halves = [slice(h * I // 2, (h + 1) * I // 2) for h in range(2)]
+        for half in halves:
+            nc.vector.tensor_copy(a_list[:, half], a_all[:].indirect(lists[:, half.start // 16 : half.stop // 16]))
         ta_all = scores("ta", dq_codes, dq_scales, False)
-        g_bf = weave("gout", g_raw, False)
+        sig = slots("sig")
+        for half in halves:
+            nc.scalar.activation(out=sig[:, half], in_=a_list[:, half], func=ACT.Sigmoid, bias=neg_th[:])
         fold = slots("fold")
-        nc.scalar.activation(out=fold[:], in_=sig[:], func=ACT.Abs, bias=-0.5)
-        ramp = slots("ramp")
-        ramp_sum = column("ramp_sum")
-        nc.scalar.activation(out=ramp[:], in_=a_list[:], func=ACT.Relu, bias=neg_th[:], accum_out=ramp_sum[:])
+        for half in halves:
+            nc.scalar.activation(out=fold[:, half], in_=sig[:, half], func=ACT.Abs, bias=-0.5)
+
+        v_bf = [weave("v%d" % c, v_raw[c]) for c in range(T // CHUNK)]
         log_part = slots("log_part")
         log_sum = column("log_sum")
         nc.scalar.activation(out=log_part[:], in_=fold[:], func=ACT.Ln, bias=0.5, accum_out=log_sum[:])
-        z_known = column("z_known")
-        nc.scalar.activation(out=z_known[:], in_=ramp_sum[:], func=ACT.Identity, bias=reserve_sb[:])
-        z_row = column("z_row")
-        nc.scalar.activation(out=z_row[:], in_=log_sum[:], func=ACT.Identity, scale=-1.0, bias=z_known[:])
-
-        g_codes, g_scales = quantise("gout", g_bf)
-        value_scores(0, *quantise("v0", weave("v0", v_raw[0], False)))
-        v_bf = [None] + [weave("v%d" % c, v_raw[c], False) for c in range(1, T // CHUNK)]
+        value_scores(0, *quantise("v0", v_bf[0], tag="v1_raw"))
         value_scores(1, *quantise("v1", v_bf[1], tag="v2_raw"))
         value_scores(2, *quantise("v2", v_bf[2], tag="v3_raw"))
         value_scores(3, *quantise("v3", v_bf[3]))
+        ramp = slots("ramp", tag="fold")
+        ramp_sum = column("ramp_sum")
+        nc.scalar.activation(out=ramp[:], in_=a_list[:], func=ACT.Relu, bias=neg_th[:], accum_out=ramp_sum[:])
+        z_known = column("z_known")
+        nc.scalar.activation(out=z_known[:], in_=log_sum[:], func=ACT.Identity, scale=-1.0, bias=reserve_sb[:])
+        z_row = column("z_row")
+        nc.scalar.activation(out=z_row[:], in_=ramp_sum[:], func=ACT.Identity, bias=z_known[:])
+        for h in range(T // BANK):
+            nc.scalar.copy(out=c0_all[:, h * BANK : (h + 1) * BANK], in_=c0_banks[h][:])
         xp = slots("xp", tag="v3_bf")
         nc.vector.tensor_tensor(xp[:], ta_all[:].indirect(lists[:]), sig[:], ALU.mult)
-        inv_z = column("inv_z", tag="ta")
+        inv_z = column("inv_z", tag="v3_codes")
         nc.vector.reciprocal(inv_z[:], z_row[:])
-        neg_p = slots("neg_p", tag="v2_bf")
-        nc.vector.tensor_tensor(neg_p[:], log_part[:], ramp[:], ALU.subtract)
+        neg_p = slots("neg_p", tag="ta")
+        nc.gpsimd.tensor_tensor(neg_p[:], log_part[:], ramp[:], ALU.subtract)
+        dw = slots("dw")
+        nc.vector.tensor_copy(dw[:], c0_all[:].indirect(lists[:]))
+        neg_curve = slots("neg_curve", tag="c0_all")
+        nc.vector.scalar_tensor_tensor(neg_curve[:], sig[:], 1.0, xp[:], ALU.subtract, ALU.mult)
         xp_share = slots("xp_share")
         xz_share = column("xz_share")
         nc.scalar.activation(out=xp_share[:], in_=xp[:], func=ACT.Copy, scale=inv_z[:], accum_out=xz_share[:])
         row_scale = column("row_scale")
         nc.scalar.activation(out=row_scale[:], in_=inv_z[:], func=ACT.Copy, scale=-1024.0)
 
-        dw = slots("dw")
-        nc.vector.tensor_copy(dw[:], c0_all[:].indirect(lists[:]))
-        neg_curve = slots("neg_curve", tag="c0_all")
-        nc.vector.scalar_tensor_tensor(neg_curve[:], sig[:], 1.0, xp[:], ALU.subtract, ALU.mult)
         scrap_a = slots("scrap_a")
         shift = column("shift")
         nc.vector.scalar_tensor_tensor(scrap_a[:], neg_p[:], inv_z[:], dw[:], ALU.mult, ALU.mult, accum_out=shift[:])

@@ -2,7 +2,7 @@ from contextlib import ExitStack
 
 import concourse.mybir as mybir
 
-D, E, T, Q, I = 512, 512, 1024, 128, 512
+D, T, Q, I = 512, 1024, 128, 512
 FLOPS = 3 * 2 * D * Q * T
 
 F32 = mybir.dt.float32
@@ -18,12 +18,19 @@ ACT = mybir.ActivationFunctionType
 
 P = 128
 PACK = 4
+LINE = 4
+GROUP = 16
 BANK = 512
 CHUNK = 256
 
 
+def two_halves(n):
+    return [slice(0, n // 2), slice(n // 2, n)]
+
+
 def tile_attend_hvspotlight_heads_kernel(tc, query, keys_words, keys_scales, gout, vals, th, reserve, dquery, base, offs, out):
     nc = tc.nc
+    chunks = [slice(c * CHUNK, (c + 1) * CHUNK) for c in range(T // CHUNK)]
     with ExitStack() as ctx:
         sb = ctx.enter_context(tc.tile_pool(name="sb", bufs=1))
         ps = ctx.enter_context(tc.psum_pool(name="ps", bufs=1))
@@ -33,64 +40,69 @@ def tile_attend_hvspotlight_heads_kernel(tc, query, keys_words, keys_scales, gou
             nc.sync.dma_start(out=raw[:], in_=src.rearrange("(p j) w -> p j w", j=PACK))
             return raw
 
-        def weave(name, raw, scalar_columns=0):
-            width = raw.shape[2]
-            woven = sb.tile([P, width, PACK], BF16, name=name + "_bf", tag=name + "_bf", align_bytes=64)
-            dst = woven[:].rearrange("p (c i) j -> p c j i", i=4)
-            src = raw[:].rearrange("p j (c i) -> p c j i", i=4)
-            cut = scalar_columns // 4
-            if cut:
-                nc.scalar.copy(out=dst[:, :cut], in_=src[:, :cut])
-            nc.vector.tensor_copy(out=dst[:, cut:], in_=src[:, cut:])
+        def weave(name, rows):
+            woven = sb.tile([P, rows.shape[2], PACK], BF16, name=name + "_bf", align_bytes=64)
+            nc.vector.tensor_copy(
+                out=woven[:].rearrange("p (c i) j -> p c j i", i=LINE),
+                in_=rows.rearrange("p j (c i) -> p c j i", i=LINE),
+            )
             return woven
 
-        def quantise(name, woven, tag=None):
-            width = woven.shape[1]
+        def quantise(name, woven_parts, tag=None):
+            part_width = woven_parts[0].shape[1]
+            width = part_width * len(woven_parts)
             codes = sb.tile([P, width], U32, name=name + "_codes", tag=tag or name + "_codes", align_bytes=64)
             scales = sb.tile([P, width], U8, name=name + "_scales", align_bytes=64)
-            nc.vector.quantize_mx(out=codes[:].bitcast(FP8X4), scales=scales[:], in_=woven[:].rearrange("p w j -> p (w j)"))
+            for n, woven in enumerate(woven_parts):
+                cols = slice(n * part_width, (n + 1) * part_width)
+                nc.vector.quantize_mx(
+                    out=codes[:, cols].bitcast(FP8X4), scales=scales[:, cols], in_=woven[:].rearrange("p w j -> p (w j)")
+                )
             return codes, scales
 
-        def column(name, tag=None):
+        def per_row(name, tag=None):
             return sb.tile([P, 1], F32, name=name, tag=tag or name, align_bytes=64)
 
-        def slots(name, tag=None):
+        def per_slot(name, tag=None):
             return sb.tile([P, I], F32, name=name, tag=tag or name, align_bytes=64)
+
+        def per_token(name):
+            return sb.tile([P, T], F32, name=name, tag=name, align_bytes=64)
 
         key_scales = sb.tile([P, T], U8, name="key_scales", align_bytes=64)
         nc.vector.memset(key_scales[:].bitcast(I32), 0)
-        for quad in range(4):
+        for quadrant in range(4):
             nc.sync.dma_start(
-                out=key_scales[32 * quad : 32 * quad + 4, :].bitcast(I32),
-                in_=keys_scales[0, 4 * quad : 4 * quad + 4, :].bitcast(I32),
+                out=key_scales[32 * quadrant : 32 * quadrant + 4, :].bitcast(I32),
+                in_=keys_scales[0, 4 * quadrant : 4 * quadrant + 4, :].bitcast(I32),
             )
-        warm = column("warm")
-        warm_out = column("warm_out")
-        nc.vector.memset(warm[:], 0.0)
-        nc.scalar.activation(out=warm_out[:], in_=warm[:], func=ACT.Sigmoid)
+        zero = per_row("zero")
+        one_half = per_row("one_half")
+        nc.vector.memset(zero[:], 0.0)
+        nc.scalar.activation(out=one_half[:], in_=zero[:], func=ACT.Sigmoid)
         q_raw = load_rows("q", query)
         key_words = sb.tile([P, 2 * T], U8, name="key_words", align_bytes=64)
         nc.sync.dma_start(out=key_words[:].bitcast(I32), in_=keys_words[0].bitcast(I32))
         dq_raw = load_rows("dq", dquery)
-        g_raw = load_rows("gout", gout)
-        v_raw = [load_rows("v0", vals[:, 0:CHUNK])]
-        lists = sb.tile([P, I // 16], U16, name="lists")
+        gout_raw = load_rows("gout", gout)
+        v_raw = [load_rows("v0", vals[:, chunks[0]])]
+        lists = sb.tile([P, I // GROUP], U16, name="lists")
         nc.sync.dma_start(lists[:], offs)
-        th_sb = column("th_sb")
+        th_sb = per_row("th_sb")
         nc.sync.dma_start(out=th_sb[:], in_=th)
-        v_raw.extend(load_rows("v%d" % c, vals[:, c * CHUNK : (c + 1) * CHUNK]) for c in range(1, T // CHUNK))
-        reserve_sb = column("reserve_sb")
+        v_raw.extend(load_rows("v%d" % c, vals[:, chunks[c]]) for c in range(1, len(chunks)))
+        reserve_sb = per_row("reserve_sb")
         nc.sync.dma_start(out=reserve_sb[:], in_=reserve)
         base_sb = sb.tile([P, T], F32, name="base_sb")
         nc.sync.dma_start(out=base_sb[:], in_=base)
 
         placed = sb.tile([P, T], F32, name="placed")
         nc.vector.memset(placed[:], 0.0)
-        neg_th = column("neg_th")
+        neg_th = per_row("neg_th")
         nc.scalar.activation(out=neg_th[:], in_=th_sb[:], func=ACT.Copy, scale=-1.0)
 
-        def scores(name, codes, scales, second_on_vector):
-            whole = sb.tile([P, T], F32, name=name, tag=name, align_bytes=64)
+        def key_scores(name, codes, scales):
+            whole = per_token(name)
             for h in range(T // BANK):
                 bank = ps.tile([P, BANK], F32, name="%s_bank%d" % (name, h))
                 nc.tensor.matmul_mx(
@@ -102,96 +114,97 @@ def tile_attend_hvspotlight_heads_kernel(tc, query, keys_words, keys_scales, gou
                     start=True,
                     stop=True,
                 )
-                if h == 1 and second_on_vector:
-                    nc.vector.tensor_copy(out=whole[:, h * BANK : (h + 1) * BANK], in_=bank[:])
-                else:
-                    nc.scalar.copy(out=whole[:, h * BANK : (h + 1) * BANK], in_=bank[:])
+                nc.scalar.copy(out=whole[:, h * BANK : (h + 1) * BANK], in_=bank[:])
             return whole
 
-        c0_all = sb.tile([P, T], F32, name="c0_all", tag="c0_all", align_bytes=64)
+        c0_all = per_token("c0_all")
+        c0_spans = [slice(0, 2 * CHUNK), chunks[2], chunks[3]]
+        c0_banks = [ps.tile([P, span.stop - span.start], F32, name="c0_bank%d" % b) for b, span in enumerate(c0_spans)]
+        c0_targets = [c0_banks[0][:, :CHUNK], c0_banks[0][:, CHUNK:], c0_banks[1][:], c0_banks[2][:]]
 
-        c0_banks = [ps.tile([P, BANK], F32, name="c0_bank%d" % h) for h in range(T // BANK)]
-
-        def value_scores(c, v_codes, v_scales):
-            h, part = divmod(c * CHUNK, BANK)
+        def value_scores(c, codes, scales):
             nc.tensor.matmul_mx(
-                out=c0_banks[h][:, part : part + CHUNK],
-                lhsT=g_codes[:].bitcast(FP8X4),
-                lhsT_scale=g_scales[:],
-                rhs=v_codes[:].bitcast(FP8X4),
-                rhs_scale=v_scales[:],
+                out=c0_targets[c],
+                lhsT=gout_codes[:].bitcast(FP8X4),
+                lhsT_scale=gout_scales[:],
+                rhs=codes[:].bitcast(FP8X4),
+                rhs_scale=scales[:],
                 start=True,
                 stop=True,
             )
 
-        q_bf = weave("q", q_raw)
-        q_codes, q_scales = quantise("q", q_bf)
-        a_all = scores("a", q_codes, q_scales, False)
-        dq_bf = weave("dq", dq_raw)
-        g_bf = weave("gout", g_raw)
-        dq_codes, dq_scales = quantise("dq", dq_bf)
-        g_codes, g_scales = quantise("gout", g_bf)
+        q_codes, q_scales = quantise("q", [weave("q", q_raw[:])])
+        a_all = key_scores("a_all", q_codes, q_scales)
+        dq_bf = weave("dq", dq_raw[:])
+        gout_bf = weave("gout", gout_raw[:])
+        dq_codes, dq_scales = quantise("dq", [dq_bf])
+        gout_codes, gout_scales = quantise("gout", [gout_bf])
 
-        a_list = slots("a_list")
-        halves = [slice(h * I // 2, (h + 1) * I // 2) for h in range(2)]
-        for half in halves:
-            nc.vector.tensor_copy(a_list[:, half], a_all[:].indirect(lists[:, half.start // 16 : half.stop // 16]))
-        ta_all = scores("ta", dq_codes, dq_scales, False)
-        sig = slots("sig")
-        for half in halves:
+        a_list = per_slot("a_list")
+        for half in two_halves(I):
+            nc.vector.tensor_copy(a_list[:, half], a_all[:].indirect(lists[:, half.start // GROUP : half.stop // GROUP]))
+        ta_all = key_scores("ta_all", dq_codes, dq_scales)
+        sig = per_slot("sig")
+        for half in two_halves(I):
             nc.scalar.activation(out=sig[:, half], in_=a_list[:, half], func=ACT.Sigmoid, bias=neg_th[:])
-        fold = slots("fold")
-        for half in halves:
-            nc.scalar.activation(out=fold[:, half], in_=sig[:, half], func=ACT.Abs, bias=-0.5)
+        off_centre = per_slot("off_centre")
+        for half in two_halves(I):
+            nc.scalar.activation(out=off_centre[:, half], in_=sig[:, half], func=ACT.Abs, bias=-0.5)
 
-        v_bf = [weave("v%d" % c, v_raw[c]) for c in range(T // CHUNK)]
-        log_part = slots("log_part")
-        log_sum = column("log_sum")
-        nc.scalar.activation(out=log_part[:], in_=fold[:], func=ACT.Ln, bias=0.5, accum_out=log_sum[:])
-        value_scores(0, *quantise("v0", v_bf[0], tag="v1_raw"))
-        value_scores(1, *quantise("v1", v_bf[1], tag="v2_raw"))
-        value_scores(2, *quantise("v2", v_bf[2], tag="v3_raw"))
-        value_scores(3, *quantise("v3", v_bf[3]))
-        ramp = slots("ramp", tag="fold")
-        ramp_sum = column("ramp_sum")
+        v0_bf = weave("v0", v_raw[0][:])
+        log_part = per_slot("log_part")
+        log_sum = per_row("log_sum")
+        nc.scalar.activation(out=log_part[:], in_=off_centre[:], func=ACT.Ln, bias=one_half[:], accum_out=log_sum[:])
+
+        value_scores(0, *quantise("v0", [v0_bf], tag="v1_raw"))
+        for c in range(1, len(chunks)):
+            parts = [weave("v%d_%d" % (c, n), v_raw[c][:, :, part]) for n, part in enumerate(two_halves(CHUNK))]
+            value_scores(c, *quantise("v%d" % c, parts))
+
+        ramp = per_slot("ramp", tag="off_centre")
+        ramp_sum = per_row("ramp_sum")
         nc.scalar.activation(out=ramp[:], in_=a_list[:], func=ACT.Relu, bias=neg_th[:], accum_out=ramp_sum[:])
-        z_known = column("z_known")
-        nc.scalar.activation(out=z_known[:], in_=log_sum[:], func=ACT.Identity, scale=-1.0, bias=reserve_sb[:])
-        z_row = column("z_row")
-        nc.scalar.activation(out=z_row[:], in_=ramp_sum[:], func=ACT.Identity, bias=z_known[:])
-        for h in range(T // BANK):
-            nc.scalar.copy(out=c0_all[:, h * BANK : (h + 1) * BANK], in_=c0_banks[h][:])
-        xp = slots("xp", tag="v3_bf")
+        nc.scalar.copy(out=c0_all[:, c0_spans[0]], in_=c0_banks[0][:])
+        nc.scalar.copy(out=c0_all[:, c0_spans[1]], in_=c0_banks[1][:])
+        nc.vector.tensor_copy(out=c0_all[:, c0_spans[2]], in_=c0_banks[2][:])
+
+        z_part = per_row("z_part", tag="v3_codes")
+        nc.scalar.activation(out=z_part[:], in_=log_sum[:], func=ACT.Identity, scale=-1.0, bias=reserve_sb[:])
+        z_row = per_row("z_row")
+        nc.scalar.activation(out=z_row[:], in_=ramp_sum[:], func=ACT.Identity, bias=z_part[:])
+        xp = per_slot("xp", tag="v3_raw")
         nc.vector.tensor_tensor(xp[:], ta_all[:].indirect(lists[:]), sig[:], ALU.mult)
-        inv_z = column("inv_z", tag="v3_codes")
-        nc.vector.reciprocal(inv_z[:], z_row[:])
-        neg_p = slots("neg_p", tag="ta")
+        neg_p = per_slot("neg_p", tag="ta_all")
         nc.gpsimd.tensor_tensor(neg_p[:], log_part[:], ramp[:], ALU.subtract)
-        dw = slots("dw")
+        dw = per_slot("dw")
         nc.vector.tensor_copy(dw[:], c0_all[:].indirect(lists[:]))
-        neg_curve = slots("neg_curve", tag="c0_all")
+        inv_z = per_row("inv_z")
+        nc.vector.reciprocal(inv_z[:], z_row[:])
+        neg_curve = per_slot("neg_curve", tag="v3_codes")
         nc.vector.scalar_tensor_tensor(neg_curve[:], sig[:], 1.0, xp[:], ALU.subtract, ALU.mult)
-        xp_share = slots("xp_share")
-        xz_share = column("xz_share")
-        nc.scalar.activation(out=xp_share[:], in_=xp[:], func=ACT.Copy, scale=inv_z[:], accum_out=xz_share[:])
-        row_scale = column("row_scale")
+        xz_terms = per_slot("xz_terms")
+        xz_share = per_row("xz_share")
+        nc.scalar.activation(out=xz_terms[:], in_=xp[:], func=ACT.Copy, scale=inv_z[:], accum_out=xz_share[:])
+        row_scale = per_row("row_scale")
         nc.scalar.activation(out=row_scale[:], in_=inv_z[:], func=ACT.Copy, scale=-1024.0)
 
-        scrap_a = slots("scrap_a")
-        shift = column("shift")
-        nc.vector.scalar_tensor_tensor(scrap_a[:], neg_p[:], inv_z[:], dw[:], ALU.mult, ALU.mult, accum_out=shift[:])
-        slope = slots("slope")
+        shift_terms = per_slot("shift_terms")
+        shift = per_row("shift")
+        nc.vector.scalar_tensor_tensor(shift_terms[:], neg_p[:], inv_z[:], dw[:], ALU.mult, ALU.mult, accum_out=shift[:])
+        dw_xp_terms = per_slot("dw_xp_terms")
+        dw_xp_share = per_row("dw_xp_share")
+        nc.vector.scalar_tensor_tensor(dw_xp_terms[:], xp[:], inv_z[:], dw[:], ALU.mult, ALU.mult, accum_out=dw_xp_share[:])
+        slope = per_slot("slope", tag="shift_terms")
         nc.vector.scalar_tensor_tensor(slope[:], sig[:], xz_share[:], neg_curve[:], ALU.mult, ALU.add)
-        scrap_b = slots("scrap_b")
-        offset = column("offset")
-        nc.vector.scalar_tensor_tensor(scrap_b[:], dw[:], shift[:], xp_share[:], ALU.add, ALU.mult, accum_out=offset[:])
-        level = slots("level")
-        nc.scalar.activation(out=level[:], in_=sig[:], func=ACT.Copy, scale=offset[:])
-        main = slots("main")
-        nc.vector.scalar_tensor_tensor(main[:], dw[:], shift[:], slope[:], ALU.add, ALU.mult)
-        nc.vector.tensor_tensor(placed[:].indirect(lists[:]), main[:], level[:], ALU.add)
+        level_factor = per_row("level_factor")
+        nc.scalar.activation(out=level_factor[:], in_=shift[:], func=ACT.Identity, scale=xz_share[:], bias=dw_xp_share[:])
+        level = per_slot("level")
+        nc.scalar.activation(out=level[:], in_=sig[:], func=ACT.Copy, scale=level_factor[:])
+        tilted = per_slot("tilted")
+        nc.vector.scalar_tensor_tensor(tilted[:], dw[:], shift[:], slope[:], ALU.add, ALU.mult)
+        nc.vector.tensor_tensor(placed[:].indirect(lists[:]), tilted[:], level[:], ALU.add)
 
-        for h, cols in enumerate((slice(0, 512), slice(512, 768), slice(768, 1024))):
-            result = sb.tile([P, cols.stop - cols.start], F32, name="result%d" % h)
+        for c, cols in enumerate(chunks):
+            result = sb.tile([P, CHUNK], F32, name="result%d" % c)
             nc.vector.scalar_tensor_tensor(result[:], placed[:, cols], row_scale[:], base_sb[:, cols], ALU.mult, ALU.add)
             nc.sync.dma_start(out=out[:, cols], in_=result[:])

from contextlib import ExitStack

import concourse.mybir as mybir

D, T, Q, I = 512, 1024, 128, 512
FLOPS = 3 * 2 * D * Q * T

F32 = mybir.dt.float32
BF16 = mybir.dt.bfloat16
I32 = mybir.dt.int32
U32 = mybir.dt.uint32
U16 = mybir.dt.uint16
U8 = mybir.dt.uint8
FP8X4 = mybir.dt.float8_e4m3fn_x4
FP4X4 = mybir.dt.float4_e2m1fn_x4
ALU = mybir.AluOpType
ACT = mybir.ActivationFunctionType

P = 128
PACK = 4
LINE = 4
GROUP = 16
BANK = 512
CHUNK = 256


def two_halves(n):
    return [slice(0, n // 2), slice(n // 2, n)]


def tile_attend_hvspotlight_heads_kernel(tc, query, keys_words, keys_scales, gout, vals, th, reserve, dquery, base, offs, out):
    nc = tc.nc
    chunks = [slice(c * CHUNK, (c + 1) * CHUNK) for c in range(T // CHUNK)]
    with ExitStack() as ctx:
        sb = ctx.enter_context(tc.tile_pool(name="sb", bufs=1))
        ps = ctx.enter_context(tc.psum_pool(name="ps", bufs=1))

        def load_rows(name, src):
            raw = sb.tile([P, PACK, src.shape[1]], F32, name=name + "_raw", tag=name + "_raw", align_bytes=64)
            nc.sync.dma_start(out=raw[:], in_=src.rearrange("(p j) w -> p j w", j=PACK))
            return raw

        def weave(name, rows):
            woven = sb.tile([P, rows.shape[2], PACK], BF16, name=name + "_bf", align_bytes=64)
            nc.vector.tensor_copy(
                out=woven[:].rearrange("p (c i) j -> p c j i", i=LINE),
                in_=rows.rearrange("p j (c i) -> p c j i", i=LINE),
            )
            return woven

        def quantise(name, woven_parts, tag=None):
            part_width = woven_parts[0].shape[1]
            width = part_width * len(woven_parts)
            codes = sb.tile([P, width], U32, name=name + "_codes", tag=tag or name + "_codes", align_bytes=64)
            scales = sb.tile([P, width], U8, name=name + "_scales", align_bytes=64)
            for n, woven in enumerate(woven_parts):
                cols = slice(n * part_width, (n + 1) * part_width)
                nc.vector.quantize_mx(
                    out=codes[:, cols].bitcast(FP8X4), scales=scales[:, cols], in_=woven[:].rearrange("p w j -> p (w j)")
                )
            return codes, scales

        def per_row(name, tag=None):
            return sb.tile([P, 1], F32, name=name, tag=tag or name, align_bytes=64)

        def per_slot(name, tag=None):
            return sb.tile([P, I], F32, name=name, tag=tag or name, align_bytes=64)

        def per_token(name):
            return sb.tile([P, T], F32, name=name, tag=name, align_bytes=64)

        key_scales = sb.tile([P, T], U8, name="key_scales", align_bytes=64)
        nc.vector.memset(key_scales[:].bitcast(I32), 0)
        for quadrant in range(4):
            nc.sync.dma_start(
                out=key_scales[32 * quadrant : 32 * quadrant + 4, :].bitcast(I32),
                in_=keys_scales[0, 4 * quadrant : 4 * quadrant + 4, :].bitcast(I32),
            )
        zero = per_row("zero")
        one_half = per_row("one_half")
        nc.vector.memset(zero[:], 0.0)
        nc.scalar.activation(out=one_half[:], in_=zero[:], func=ACT.Sigmoid)
        q_raw = load_rows("q", query)
        key_words = sb.tile([P, 2 * T], U8, name="key_words", align_bytes=64)
        nc.sync.dma_start(out=key_words[:].bitcast(I32), in_=keys_words[0].bitcast(I32))
        dq_raw = load_rows("dq", dquery)
        gout_raw = load_rows("gout", gout)
        v_raw = [load_rows("v0", vals[:, chunks[0]])]
        lists = sb.tile([P, I // GROUP], U16, name="lists")
        nc.sync.dma_start(lists[:], offs)
        th_sb = per_row("th_sb")
        nc.sync.dma_start(out=th_sb[:], in_=th)
        v_raw.extend(load_rows("v%d" % c, vals[:, chunks[c]]) for c in range(1, len(chunks)))
        reserve_sb = per_row("reserve_sb")
        nc.sync.dma_start(out=reserve_sb[:], in_=reserve)
        base_sb = sb.tile([P, T], F32, name="base_sb")
        nc.sync.dma_start(out=base_sb[:], in_=base)

        placed = sb.tile([P, T], F32, name="placed")
        nc.vector.memset(placed[:], 0.0)
        neg_th = per_row("neg_th")
        nc.scalar.activation(out=neg_th[:], in_=th_sb[:], func=ACT.Copy, scale=-1.0)

        def key_scores(name, codes, scales):
            whole = per_token(name)
            for h in range(T // BANK):
                bank = ps.tile([P, BANK], F32, name="%s_bank%d" % (name, h))
                nc.tensor.matmul_mx(
                    out=bank[:],
                    lhsT=codes[:].bitcast(FP8X4),
                    lhsT_scale=scales[:],
                    rhs=key_words[:, 2 * h * BANK : 2 * (h + 1) * BANK].bitcast(FP4X4),
                    rhs_scale=key_scales[:, h * BANK : (h + 1) * BANK],
                    start=True,
                    stop=True,
                )
                nc.scalar.copy(out=whole[:, h * BANK : (h + 1) * BANK], in_=bank[:])
            return whole

        c0_all = per_token("c0_all")
        c0_spans = [slice(0, 2 * CHUNK), chunks[2], chunks[3]]
        c0_banks = [ps.tile([P, span.stop - span.start], F32, name="c0_bank%d" % b) for b, span in enumerate(c0_spans)]
        c0_targets = [c0_banks[0][:, :CHUNK], c0_banks[0][:, CHUNK:], c0_banks[1][:], c0_banks[2][:]]

        def value_scores(c, codes, scales):
            nc.tensor.matmul_mx(
                out=c0_targets[c],
                lhsT=gout_codes[:].bitcast(FP8X4),
                lhsT_scale=gout_scales[:],
                rhs=codes[:].bitcast(FP8X4),
                rhs_scale=scales[:],
                start=True,
                stop=True,
            )

        q_codes, q_scales = quantise("q", [weave("q", q_raw[:])])
        a_all = key_scores("a_all", q_codes, q_scales)
        dq_bf = weave("dq", dq_raw[:])
        gout_bf = weave("gout", gout_raw[:])
        dq_codes, dq_scales = quantise("dq", [dq_bf])
        gout_codes, gout_scales = quantise("gout", [gout_bf])

        a_list = per_slot("a_list")
        for half in two_halves(I):
            nc.vector.tensor_copy(a_list[:, half], a_all[:].indirect(lists[:, half.start // GROUP : half.stop // GROUP]))
        ta_all = key_scores("ta_all", dq_codes, dq_scales)
        sig = per_slot("sig")
        for half in two_halves(I):
            nc.scalar.activation(out=sig[:, half], in_=a_list[:, half], func=ACT.Sigmoid, bias=neg_th[:])
        off_centre = per_slot("off_centre")
        for half in two_halves(I):
            nc.scalar.activation(out=off_centre[:, half], in_=sig[:, half], func=ACT.Abs, bias=-0.5)

        v0_bf = weave("v0", v_raw[0][:])
        log_part = per_slot("log_part")
        log_sum = per_row("log_sum")
        nc.scalar.activation(out=log_part[:], in_=off_centre[:], func=ACT.Ln, bias=one_half[:], accum_out=log_sum[:])

        value_scores(0, *quantise("v0", [v0_bf], tag="v1_raw"))
        for c in range(1, len(chunks)):
            parts = [weave("v%d_%d" % (c, n), v_raw[c][:, :, part]) for n, part in enumerate(two_halves(CHUNK))]
            value_scores(c, *quantise("v%d" % c, parts))

        ramp = per_slot("ramp", tag="off_centre")
        ramp_sum = per_row("ramp_sum")
        nc.scalar.activation(out=ramp[:], in_=a_list[:], func=ACT.Relu, bias=neg_th[:], accum_out=ramp_sum[:])
        nc.scalar.copy(out=c0_all[:, c0_spans[0]], in_=c0_banks[0][:])
        nc.scalar.copy(out=c0_all[:, c0_spans[1]], in_=c0_banks[1][:])
        nc.vector.tensor_copy(out=c0_all[:, c0_spans[2]], in_=c0_banks[2][:])

        z_part = per_row("z_part", tag="v3_codes")
        nc.scalar.activation(out=z_part[:], in_=log_sum[:], func=ACT.Identity, scale=-1.0, bias=reserve_sb[:])
        z_row = per_row("z_row")
        nc.scalar.activation(out=z_row[:], in_=ramp_sum[:], func=ACT.Identity, bias=z_part[:])
        xp = per_slot("xp", tag="v3_raw")
        nc.vector.tensor_tensor(xp[:], ta_all[:].indirect(lists[:]), sig[:], ALU.mult)
        neg_p = per_slot("neg_p", tag="ta_all")
        nc.gpsimd.tensor_tensor(neg_p[:], log_part[:], ramp[:], ALU.subtract)
        dw = per_slot("dw")
        nc.vector.tensor_copy(dw[:], c0_all[:].indirect(lists[:]))
        inv_z = per_row("inv_z")
        nc.vector.reciprocal(inv_z[:], z_row[:])
        neg_curve = per_slot("neg_curve", tag="v3_codes")
        nc.vector.scalar_tensor_tensor(neg_curve[:], sig[:], 1.0, xp[:], ALU.subtract, ALU.mult)
        xz_terms = per_slot("xz_terms")
        xz_share = per_row("xz_share")
        nc.scalar.activation(out=xz_terms[:], in_=xp[:], func=ACT.Copy, scale=inv_z[:], accum_out=xz_share[:])
        row_scale = per_row("row_scale")
        nc.scalar.activation(out=row_scale[:], in_=inv_z[:], func=ACT.Copy, scale=-1024.0)

        shift_terms = per_slot("shift_terms")
        shift = per_row("shift")
        nc.vector.scalar_tensor_tensor(shift_terms[:], neg_p[:], inv_z[:], dw[:], ALU.mult, ALU.mult, accum_out=shift[:])
        dw_xp_terms = per_slot("dw_xp_terms")
        dw_xp_share = per_row("dw_xp_share")
        nc.vector.scalar_tensor_tensor(dw_xp_terms[:], xp[:], inv_z[:], dw[:], ALU.mult, ALU.mult, accum_out=dw_xp_share[:])
        slope = per_slot("slope", tag="shift_terms")
        nc.vector.scalar_tensor_tensor(slope[:], sig[:], xz_share[:], neg_curve[:], ALU.mult, ALU.add)
        level_factor = per_row("level_factor")
        nc.scalar.activation(out=level_factor[:], in_=shift[:], func=ACT.Identity, scale=xz_share[:], bias=dw_xp_share[:])
        level = per_slot("level")
        nc.scalar.activation(out=level[:], in_=sig[:], func=ACT.Copy, scale=level_factor[:])
        tilted = per_slot("tilted")
        nc.vector.scalar_tensor_tensor(tilted[:], dw[:], shift[:], slope[:], ALU.add, ALU.mult)
        nc.vector.tensor_tensor(placed[:].indirect(lists[:]), tilted[:], level[:], ALU.add)

        for c, cols in enumerate(chunks):
            result = sb.tile([P, CHUNK], F32, name="result%d" % c)
            nc.vector.scalar_tensor_tensor(result[:], placed[:, cols], row_scale[:], base_sb[:, cols], ALU.mult, ALU.add)
            nc.sync.dma_start(out=out[:, cols], in_=result[:])
